import numpy as np, ml_dtypes
CORES = [23,119,17,113]
N = 4
import mx_ref
BF = ml_dtypes.bfloat16
def f(rng, *shape):
    return mx_ref.flush((rng.standard_normal(shape, dtype=np.float32) * np.exp2(rng.integers(-2, 3, shape[:-1] + (1,)))).astype(BF))
def wide(rng, *shape, cols=0):
    v = rng.standard_normal(shape, dtype=np.float32) * np.exp2(rng.integers(-12, 13, shape)).astype(np.float32)
    if cols: v *= np.repeat(np.exp2(rng.integers(-cols, cols + 1, shape[:-2] + (1, shape[-1] // 4))) * (rng.random(shape[:-2] + (1, shape[-1] // 4)) > 0.0625), 4, axis=-1).astype(np.float32)
    return mx_ref.flush(v.astype(BF))
R, XC = 2048, 384
def lists(rng):
    return rng.integers(0, R, (N, N, 512))
def picks(L):
    return np.ascontiguousarray(L.reshape(N, N, 128, 4).transpose(0, 2, 1, 3)).reshape(N, 128, 4 * N).astype(np.int32)
def setup_inputs(rng):
    return {"x": f(rng, N, R, XC), "w": f(rng, N, R, 128), "pick": picks(lists(rng))}
def setup_inputs_alike(rng):
    d = setup_inputs(rng); L = lists(rng)
    L[:] = L[0, 0].copy()
    d["pick"] = picks(L); return d
def setup_inputs_giant(rng):
    d = setup_inputs(rng); L = lists(rng); big = {}
    for n in ("x", "w"):
        big[n] = 32 * np.arange(R // 32) + rng.integers(0, 32, (N, R // 32))
        m = np.ones((N, R, 1), np.float32)
        for r in range(N): m[r, big[n][r]] = 4096
        d[n] = (d[n].astype(np.float32) * m).astype(BF)
    for r in range(N):
        for s in range(N):
            for g in range(16):
                a, b = 32 * g + rng.permutation(32)[:2]
                L[r, s, a] = rng.choice(big["x"][s]); L[r, s, b] = rng.choice(big["w"][r])
    d["pick"] = picks(L); return d
def setup_inputs_repeat(rng):
    d = setup_inputs(rng); L = lists(rng)
    for r in range(N): L[r, (r + rng.integers(1, N)) % N] = rng.integers(0, R)
    d["pick"] = picks(L); return d
def setup_inputs_sorted(rng):
    d = setup_inputs(rng); L = lists(rng)
    L[:, :, 0] = 0; L[:, :, 1] = R - 1
    d["pick"] = picks(np.sort(L, axis=2)); return d
def setup_inputs_spread(rng):
    d = setup_inputs(rng); d["x"] = wide(rng, N, R, XC); d["w"] = wide(rng, N, R, 128); return d
def check_inputs(d):
    b = []
    for n in ("x", "w"):
        a = np.abs(np.asarray(d[n]).astype(np.float32))
        if not np.isfinite(a).all() or ((a != 0) & ((a < 2.0 ** -30) | (a > 2.0 ** 30))).any(): b.append(n)
    if d["pick"].min() < 0 or d["pick"].max() >= R: b.append("pick")
    return b
def rowtile(v, k):
    return np.ascontiguousarray(v[k].transpose(0, 2, 1)).reshape(128, -1)
def reference(x, w, pick):
    y = np.zeros((N, 128, N * XC), np.float32)
    for r in range(N):
        for s in range(N):
            k = pick[r][:, 4 * s:4 * s + 4]
            y[r][:, XC * s:XC * s + XC] = mx_ref.matmul(mx_ref.quantize(rowtile(w[r], k)), mx_ref.quantize(rowtile(x[s], k)))
    return {"y": y}

@@ -1,0 +1,307 @@
+from concourse.bass import DstId, IndirectOffsetOnAxis, RemoteDMATransfer
+from concourse.mybir import dt, AluOpType, ActivationFunctionType
+
+N, R, XC = 4, 2048, 384
+COPY = ActivationFunctionType.Copy
+XW = 6144
+XSLOT = 768
+WSLOT = 512
+
+SCRATCH = {
+    "ones": ("sbuf", [128, 128], "float32"),
+    "ident": ("sbuf", [128, 128], "float32"),
+    "part": ("sbuf", [128, 1], "int32"),
+    "hbit": ("sbuf", [128, 1], "int32"),
+    "m1": ("sbuf", [128, 1], "float32"),
+    "m0": ("sbuf", [128, 1], "float32"),
+    "pk": ("sbuf", [128, 16], "int32"),
+    "ld": ("sbuf", [128, 4], "int32"),
+    "la": ("sbuf", [128, 8], "int32"),
+    "nat": ("sbuf", [128, 48, 128], "bfloat16"),
+    "stg": ("sbuf", [128, XW], "bfloat16"),
+    "xw": ("sbuf", [128, XW], "bfloat16"),
+    "wn": ("sbuf", [128, 16, 128], "bfloat16"),
+    "wst": ("sbuf", [128, 2048], "bfloat16"),
+    "ww": ("sbuf", [128, 2048], "bfloat16"),
+    "wt": ("sbuf", [128, 2048], "bfloat16"),
+    "wq": ("sbuf", [128, 512], "float8_e4m3fn_x4"),
+    "ws": ("sbuf", [128, 512], "uint8"),
+    "ysb": ("sbuf", [128, 1536], "float32"),
+    "pX": ("psum", [128, 1536], "float32"),
+    "pW": ("psum", [128, 1024], "float32"),
+    "pL": ("psum", [128, 512], "float32"),
+    "pY": ("psum", [128, 1024], "float32"),
+}
+for _l, _n in (("ow", 4), ("ax", 2)):
+    for _b in ("a1", "b1", "k1"):
+        SCRATCH[_l + _b] = ("sbuf", [128, _n, 4], "int32")
+    for _b in ("f1", "f2", "f3"):
+        SCRATCH[_l + _b] = ("sbuf", [128, _n, 4], "float32")
+    SCRATCH[_l + "u"] = ("sbuf", [128, 16 // _n, _n, 4, 2], "float32")
+    for _b in ("e0", "e1", "t2"):
+        SCRATCH[_l + _b] = ("sbuf", [128, 4, 2, 16], "float32")
+    SCRATCH[_l + "z"] = ("sbuf", [128, 4, 32], "float32")
+    SCRATCH[_l + "om"] = ("sbuf", [128, _n, 4, 4, 2], "uint16")
+    SCRATCH[_l + "off"] = ("sbuf", [128, 32 * _n], "uint16")
+for _k in range(2):
+    for _b in range(3):
+        SCRATCH["gx%d%d" % (_k, _b)] = ("sbuf", [128, 512], "float32")
+    SCRATCH["xg%d" % _k] = ("sbuf", [128, 4 * XC], "bfloat16")
+for _k in range(4):
+    SCRATCH["gw%d" % _k] = ("sbuf", [128, 512], "float32")
+    SCRATCH["xt%d" % _k] = ("sbuf", [128, 4 * XC], "bfloat16")
+    SCRATCH["xq%d" % _k] = ("sbuf", [128, XC], "float8_e4m3fn_x4")
+    SCRATCH["xs%d" % _k] = ("sbuf", [128, XC], "uint8")
+for _k in range(3):
+    SCRATCH["rq%d" % _k] = ("sbuf", [128, XC], "float8_e4m3fn_x4")
+    SCRATCH["rs%d" % _k] = ("sbuf", [128, XC], "uint8")
+
+SEMAPHORES = (["V", "S", "P", "G", "sent", "lpk", "lxa", "lxb", "lw", "wsh"]
+              + ["xsh%d%d" % (c, q) for c in range(2) for q in range(2)]
+              + ["list%d" % k for k in range(3)] + ["arr%d" % k for k in range(3)]
+              + ["ig%d%d" % (k, t) for k in range(2) for t in range(4)]
+              + ["ys%d" % k for k in range(4)])
+
+
+def roles(core, T, topo):
+    me = T.rank_of(core)
+    far = [s for s in range(N) if topo.chip(T.cores[s]) != topo.chip(core)]
+    far.sort(key=lambda s: topo.die(T.cores[s]) != topo.die(core))
+    return far + [s for s in range(N) if s != me and s not in far]
+
+
+def rank_program(g, core, T, topo):
+    me = T.rank_of(core)
+    if me is None:
+        return
+    Q = {"V": g.vector, "S": g.scalar, "P": g.tensor, "G": g, "Y": g.sync}
+    count = {"V": 0, "S": 0, "P": 0, "G": 0}
+    seen = {}
+
+    def wait(q, *toks):
+        for name, val in toks:
+            if seen.get((q, name), 0) < val:
+                seen[(q, name)] = val
+                Q[q].wait_ge(T.sem[name], val)
+
+    def tick(q, ins):
+        count[q] += 1
+        ins.then_inc(T.sem[q], 1)
+        return (q, count[q])
+
+    def now(q):
+        return (q, count[q])
+
+    v, sc, pe, sy = g.vector, g.scalar, g.tensor, g.sync
+    D = roles(core, T, topo)
+    cores = T.cores
+
+    sc.dma_start(T.pk[:], T.pick[:]).then_inc(T.sem.lpk, 16)
+    sy.dma_start(T.nat[:, 0:24, :], T.x[0:1024, :]).then_inc(T.sem.lxa, 16)
+    sy.dma_start(T.nat[:, 24:48, :], T.x[1024:2048, :]).then_inc(T.sem.lxb, 16)
+    sy.dma_start(T.wn[:], T.w[:]).then_inc(T.sem.lw, 16)
+    PK, LX, LW = ("lpk", 16), [("lxa", 16), ("lxb", 16)], ("lw", 16)
+
+    t_ones = tick("V", v.memset(T.ones[:], 1.0))
+    t_part = tick("G", g.iota(T.part[:], [[0, 1]], 0, 1))
+    wait("G", t_ones)
+    t_id = tick("G", g.affine_select(T.ident[:], T.ones[:], [[-1, 128]], AluOpType.is_equal, 0.0, 0, 1))
+    wait("V", t_part)
+    a = tick("V", v.tensor_scalar(T.hbit[:], T.part[:], 0, 1, AluOpType.arith_shift_right, AluOpType.bitwise_and))
+    wait("V", a)
+    tick("V", v.tensor_scalar(T.m1[:], T.hbit[:], 1.0, None, AluOpType.mult))
+    tick("V", v.tensor_scalar(T.m0[:], T.hbit[:], -1.0, 1.0, AluOpType.mult, AluOpType.add))
+
+    eng = [topo.engines(core, cores[s]) for s in D]
+    picks = [eng[0][0:4], eng[1][4:8], eng[2][8:16]]
+    trs = []
+    for k, s in enumerate(D):
+        rid, pid, _ = topo.addr(cores[s])
+        dst = T.ld[:] if k == 0 else T.la[:, 4 * (k - 1):4 * k]
+        trs.append(RemoteDMATransfer(dst_ids=[DstId(rid=rid, pnc=pid)], dma_engine_mask=sum(1 << e for e in picks[k]),
+                                     remote_sem=T.sem["list%d" % k], src=T.pk[:, 4 * s:4 * s + 4], dst=dst))
+    wait("G", PK)
+    g.remote_dma_fused(trs, local_sem=T.sem.sent)
+    sent = sum(len(e) for e in picks)
+    LIST = [("list%d" % k, len(picks[k])) for k in range(3)]
+
+    def gather(k, idx, t):
+        g.indirect_dma_start(T["xg%d" % k][:, XC * t:XC * t + XC], None, T.x[:],
+                             IndirectOffsetOnAxis(ap=idx, axis=0), bounds_check=R - 1).then_inc(T.sem["ig%d%d" % (k, t)], 16)
+
+    def own(t):
+        gather(1, T.pk[:, 4 * me + t:4 * me + t + 1], t)
+
+    own(0)
+    own(1)
+    wait("G", LIST[0])
+    for t in range(4):
+        gather(0, T.ld[:, t:t + 1], t)
+    own(2)
+
+    def list_front(p, src, n, hi, lo, sh, mul, s3):
+        b = lambda x: T[p + x]
+        tick("V", v.tensor_scalar(b("a1")[:], src, hi, None, AluOpType.bitwise_and))
+        tick("V", v.tensor_scalar(b("b1")[:], src, lo, None, AluOpType.bitwise_and))
+        tick("V", v.tensor_scalar(b("k1")[:], src, sh, 31, AluOpType.arith_shift_right, AluOpType.bitwise_and))
+        wait("V", now("V"))
+        tick("V", v.tensor_scalar(b("f1")[:], b("a1")[:], float(s3), None, AluOpType.mult))
+        tick("V", v.tensor_scalar(b("f2")[:], b("b1")[:], float(mul), None, AluOpType.mult))
+        wait("V", now("V"))
+        tick("V", v.tensor_tensor(b("f3")[:], b("f1")[:], b("f2")[:], AluOpType.add))
+        wait("V", now("V"))
+        for h in range(2):
+            tick("V", v.tensor_tensor(b("u")[:, 0, :, :, h], b("f3")[:], b("k1")[:], AluOpType.add))
+        w = 1
+        while w < 16 // n:
+            wait("V", now("V"))
+            tick("V", v.tensor_copy(b("u")[:, w:2 * w], b("u")[:, 0:w]))
+            w *= 2
+        wait("P", now("V"), t_id)
+        return tick("P", pe.transpose(T.pL[:, 0:128], b("u")[:], T.ident[:]))
+
+    def list_back(p, n, tok):
+        b = lambda x: T[p + x]
+        wait("V", tok)
+        tick("V", v.tensor_scalar(b("e0")[:], T.pL[:, 0:128], T.m0[:], None, AluOpType.mult))
+        tick("V", v.tensor_scalar(b("e1")[:], T.pL[:, 0:128], T.m1[:], None, AluOpType.mult))
+        wait("V", now("V"))
+        for h in range(2):
+            tick("V", v.tensor_tensor(b("t2")[:, :, h, :], b("e0")[:, :, 0, :], b("e1")[:, :, 1, :], AluOpType.add))
+        wait("V", now("V"))
+        tick("V", v.transpose(b("z")[:], b("t2")[:]))
+        wait("V", now("V"))
+        for q in range(4):
+            tick("V", v.tensor_copy(b("om")[:, :, :, q, :], b("z")[:, q, 0:8 * n]))
+        wait("V", now("V"))
+        tick("V", v.tensor_copy(b("off")[:], b("om")[:]))
+        return now("V")
+
+    def turn_x(c):
+        wait("V", LX[c])
+        toks = []
+        for q in range(4):
+            o = (4 * c + q) * XSLOT
+            toks.append(tick("V", v.transpose(T.stg[:, o:o + XSLOT], T.nat[:, 24 * c:24 * c + 24, 32 * q:32 * q + 32])))
+        for q in range(4):
+            for a in range(4):
+                d = a % 2
+                qq = ("Y", "S")[d]
+                wait(qq, toks[q])
+                Q[qq].dma_start(T.xw[32 * q:32 * q + 32, (4 * c + a) * XSLOT:(4 * c + a + 1) * XSLOT],
+                                T.stg[32 * a:32 * a + 32, (4 * c + q) * XSLOT:(4 * c + q + 1) * XSLOT]
+                                ).then_inc(T.sem["xsh%d%d" % (c, d)], 16)
+
+    def turn_w():
+        wait("V", LW)
+        for q in range(4):
+            tick("V", v.transpose(T.wst[:, q * WSLOT:q * WSLOT + WSLOT], T.wn[:, :, 32 * q:32 * q + 32]))
+        wait("Y", now("V"))
+        for q in range(4):
+            for a in range(4):
+                sy.dma_start(T.ww[32 * q:32 * q + 32, a * WSLOT:(a + 1) * WSLOT],
+                             T.wst[32 * a:32 * a + 32, q * WSLOT:(q + 1) * WSLOT]).then_inc(T.sem.wsh, 16)
+
+    wait("V", PK)
+    tw = list_front("ow", T.pk[:], 4, 0x600, 15, 4, 32, 1)
+    turn_x(0)
+    t_offw = list_back("ow", 4, tw)
+    turn_x(1)
+    turn_w()
+    wait("V", LIST[1], LIST[2])
+    wait("P", t_offw)
+    tx = list_front("ax", T.la[:], 2, 0x700, 7, 3, 96, 3)
+    t_offx = list_back("ax", 2, tx)
+    XSH = [("xsh%d%d" % (c, d), 128) for c in range(2) for d in range(2)]
+    WSH = ("wsh", 256)
+
+    def take(q, out, win, off):
+        if q == "V":
+            return tick("V", v.tensor_copy(out, win.indirect(off)))
+        return tick("S", sc.activation(out, win.indirect(off), COPY))
+
+    def copy(q, out, in_):
+        if q == "V":
+            return tick("V", v.tensor_copy(out, in_))
+        return tick("S", sc.activation(out, in_, COPY))
+
+    free = {}
+
+    def through(q, ps, bank, buf, tok, out):
+        key = (ps, bank)
+        wait("P", t_id, tok, *([free[key]] if key in free else []))
+        for t in range(4):
+            tick("P", pe.transpose(T[ps][:, 512 * bank + t:512 * bank + 512:4], buf[:, 128 * t:128 * t + 128], T.ident[:]))
+        wait(q, now("P"))
+        free[key] = copy(q, out, T[ps][:, 512 * bank:512 * bank + 512])
+        return free[key]
+
+    def xtake(q, k, b):
+        wait(q, t_offx, *XSH)
+        return take(q, T["gx%d%d" % (k, b)][:], T.xw[:, 32 * b:32 * b + XW - 64], T.axoff[:, 32 * k:32 * k + 32])
+
+    def wtake(q, k):
+        wait(q, t_offw, WSH)
+        return take(q, T["gw%d" % k][:], T.ww[:], T.owoff[:, 32 * k:32 * k + 32])
+
+    def xthrough(q, k, b, bank, tok):
+        return through(q, "pX", bank, T["gx%d%d" % (k, b)], tok, T["xt%d" % (k + 1)][:, 512 * b:512 * b + 512])
+
+    def lace(k, buf, t):
+        wait("V", ("ig%d%d" % (buf, t), 16))
+        return tick("V", v.tensor_copy(T["xt%d" % k][:, t:4 * XC:4], T["xg%d" % buf][:, XC * t:XC * t + XC]))
+
+    def quant(k, *toks):
+        wait("V", *toks)
+        return tick("V", v.quantize_mx(T["xq%d" % k][:], T["xs%d" % k][:], T["xt%d" % k][:]))
+
+    gs = [xtake("S", 0, 0), xtake("S", 0, 1)]
+    gv = [xtake("V", 1, b) for b in range(3)]
+    for t in range(3):
+        lace(0, 0, t)
+    xthrough("S", 0, 0, 0, gs[0])
+    gs.append(xtake("S", 0, 2))
+    xthrough("V", 1, 0, 1, gv[0])
+    xthrough("S", 0, 1, 2, gs[1])
+    xthrough("V", 1, 1, 0, gv[1])
+    q0 = quant(0, lace(0, 0, 3))
+    q1 = quant(1, xthrough("S", 0, 2, 1, gs[2]))
+    q2 = quant(2, xthrough("V", 1, 2, 2, gv[2]))
+
+    for k, tok in enumerate((q0, q1, q2)):
+        c = cores[D[k]]
+        rid, pid, _ = topo.addr(c)
+        wait("G", tok)
+        g.remote_dma(T["rq%d" % k][:].bitcast(dt.uint8), T["xq%d" % k][:].bitcast(dt.uint8), T.sem["arr%d" % k], T.sem.sent,
+                     pid, rid, topo.mask(core, c))
+        g.remote_dma(T["rs%d" % k][:], T["xs%d" % k][:], T.sem["arr%d" % k], T.sem.sent, pid, rid, topo.mask(core, c))
+        sent += 2 * len(eng[k])
+    own(3)
+
+    tw = [wtake("S", k) for k in range(4)]
+    for t in range(3):
+        lace(3, 1, t)
+    tiles = [through("V", "pW", k % 2, T["gw%d" % k], tw[k], T.wt[:, 512 * k:512 * k + 512]) for k in range(4)]
+    wait("V", *tiles)
+    qw = tick("V", v.quantize_mx(T.wq[:], T.ws[:], T.wt[:]))
+    q3 = quant(3, lace(3, 1, 3))
+
+    for i, k in enumerate((2, 0, 3, 1)):
+        s = (D + [me])[k]
+        if k == 3:
+            xq, xs, tok = T.xq3, T.xs3, q3
+        else:
+            xq, xs, tok = T["rq%d" % k], T["rs%d" % k], ("arr%d" % k, 2 * len(eng[k]))
+        bank = 512 * (i % 2)
+        wait("P", qw, tok, *([free[("pY", bank)]] if i > 1 else []))
+        m = tick("P", pe.matmul_mx(T.pY[:, bank:bank + XC], T.wq[:, 128 * s:128 * s + 128], T.ws[:, 128 * s:128 * s + 128],
+                                   xq[:], xs[:], True, True))
+        q = "SV"[i % 2]
+        wait(q, m)
+        free[("pY", bank)] = e = copy(q, T.ysb[:, XC * s:XC * s + XC], T.pY[:, bank:bank + XC])
+        wait("Y", e)
+        sy.dma_start(T.y[:, XC * s:XC * s + XC], T.ysb[:, XC * s:XC * s + XC]).then_inc(T.sem["ys%d" % i], 16)
+    for i in range(4):
+        wait("Y", ("ys%d" % i, 16))
+    wait("Y", now("V"), now("S"), now("P"), now("G"))
+    wait("G", ("sent", sent))

@@ -7,16 +7,21 @@ XW = 6144
 XSLOT = 768
 WSLOT = 512
 
+PLAN = """
+G:o1 G:i0 G:o0 G:o2
+Y:lw S:g12 P:p12 S:g20 V:g10 V:tw S:g22 V:g21 S:g11 P:p10 V:l00 P:p11 S:e10 V:m2 V:e11 S:l01 V:l02
+S:gw0 P:pw0 V:l03 S:gw1 V:q0 G:s0 V:ew0 V:e12 S:gw3 P:pw1 V:q1 P:pw3 S:l31 S:gw2 Y:cw S:l30 V:ew1 P:pw2
+Y:d2 V:ew3 V:q2 G:o3 S:l32 V:ew2 S:l33 V:qw S:y0 G:s1 V:q3 V:y3 V:y1 V:y2 G:s2
+"""
+
 SCRATCH = {
     "ones": ("sbuf", [128, 128], "float32"),
     "ident": ("sbuf", [128, 128], "float32"),
-    "part": ("sbuf", [128, 1], "int32"),
-    "hbit": ("sbuf", [128, 1], "int32"),
-    "m1": ("sbuf", [128, 1], "float32"),
-    "m0": ("sbuf", [128, 1], "float32"),
     "pk": ("sbuf", [128, 16], "int32"),
     "ld": ("sbuf", [128, 4], "int32"),
-    "la": ("sbuf", [128, 8], "int32"),
+    "la": ("sbuf", [128, 2, 4], "float32"),
+    "fx": ("sbuf", [128, 16], "float32"),
+    "fw": ("sbuf", [128, 16], "float32"),
     "nat": ("sbuf", [128, 48, 128], "bfloat16"),
     "stg": ("sbuf", [128, XW], "bfloat16"),
     "xw": ("sbuf", [128, XW], "bfloat16"),
@@ -26,37 +31,36 @@ SCRATCH = {
     "wt": ("sbuf", [128, 2048], "bfloat16"),
     "wq": ("sbuf", [128, 512], "float8_e4m3fn_x4"),
     "ws": ("sbuf", [128, 512], "uint8"),
+    "gb": ("sbuf", [128, 3, 512], "bfloat16"),
+    "mv": ("sbuf", [128, 3, 4, 32, 4], "bfloat16"),
     "ysb": ("sbuf", [128, 1536], "float32"),
     "pX": ("psum", [128, 1536], "float32"),
     "pW": ("psum", [128, 1024], "float32"),
     "pL": ("psum", [128, 512], "float32"),
     "pY": ("psum", [128, 1024], "float32"),
 }
-for _l, _n in (("ow", 4), ("ax", 2)):
-    for _b in ("a1", "b1", "k1"):
-        SCRATCH[_l + _b] = ("sbuf", [128, _n, 4], "int32")
-    for _b in ("f1", "f2", "f3"):
-        SCRATCH[_l + _b] = ("sbuf", [128, _n, 4], "float32")
-    SCRATCH[_l + "u"] = ("sbuf", [128, 16 // _n, _n, 4, 2], "float32")
-    for _b in ("e0", "e1", "t2"):
-        SCRATCH[_l + _b] = ("sbuf", [128, 4, 2, 16], "float32")
-    SCRATCH[_l + "z"] = ("sbuf", [128, 4, 32], "float32")
-    SCRATCH[_l + "om"] = ("sbuf", [128, _n, 4, 4, 2], "uint16")
+for _b in ("xa", "xb", "xk", "wa", "wb", "wk"):
+    SCRATCH[_b] = ("sbuf", [128, 16], "int32")
+for _b in ("x1", "x2", "x3", "w1", "w2", "w3"):
+    SCRATCH[_b] = ("sbuf", [128, 16], "float32")
+for _l, _n in (("o", 4), ("a", 2)):
+    SCRATCH[_l + "u"] = ("sbuf", [128, 4, 8, 4], "float32")
+    SCRATCH[_l + "d"] = ("sbuf", [128, 8, 2, 16], "float32")
+    SCRATCH[_l + "z"] = ("sbuf", [128, 32, 8], "float32")
     SCRATCH[_l + "off"] = ("sbuf", [128, 32 * _n], "uint16")
 for _k in range(2):
-    for _b in range(3):
-        SCRATCH["gx%d%d" % (_k, _b)] = ("sbuf", [128, 512], "float32")
     SCRATCH["xg%d" % _k] = ("sbuf", [128, 4 * XC], "bfloat16")
+for _b in range(3):
+    SCRATCH["gx%d" % _b] = ("sbuf", [128, 512], "float32")
+    SCRATCH["rq%d" % _b] = ("sbuf", [128, XC], "float8_e4m3fn_x4")
+    SCRATCH["rs%d" % _b] = ("sbuf", [128, XC], "uint8")
 for _k in range(4):
     SCRATCH["gw%d" % _k] = ("sbuf", [128, 512], "float32")
-    SCRATCH["xt%d" % _k] = ("sbuf", [128, 4 * XC], "bfloat16")
+    SCRATCH["xt%d" % _k] = ("sbuf", [128, 3, 512] if _k == 2 else [128, 4 * XC], "bfloat16")
     SCRATCH["xq%d" % _k] = ("sbuf", [128, XC], "float8_e4m3fn_x4")
     SCRATCH["xs%d" % _k] = ("sbuf", [128, XC], "uint8")
-for _k in range(3):
-    SCRATCH["rq%d" % _k] = ("sbuf", [128, XC], "float8_e4m3fn_x4")
-    SCRATCH["rs%d" % _k] = ("sbuf", [128, XC], "uint8")
 
-SEMAPHORES = (["V", "S", "P", "G", "sent", "lpk", "lxa", "lxb", "lw", "wsh"]
+SEMAPHORES = (["V", "S", "P", "G", "sent", "lpk", "lxa", "lxb", "lw", "wsh", "xm"]
               + ["xsh%d%d" % (c, q) for c in range(2) for q in range(2)]
               + ["list%d" % k for k in range(3)] + ["arr%d" % k for k in range(3)]
               + ["ig%d%d" % (k, t) for k in range(2) for t in range(4)]
@@ -95,87 +99,82 @@ def rank_program(g, core, T, topo):
     v, sc, pe, sy = g.vector, g.scalar, g.tensor, g.sync
     D = roles(core, T, topo)
     cores = T.cores
+    A = AluOpType
 
     sc.dma_start(T.pk[:], T.pick[:]).then_inc(T.sem.lpk, 16)
     sy.dma_start(T.nat[:, 0:24, :], T.x[0:1024, :]).then_inc(T.sem.lxa, 16)
     sy.dma_start(T.nat[:, 24:48, :], T.x[1024:2048, :]).then_inc(T.sem.lxb, 16)
-    sy.dma_start(T.wn[:], T.w[:]).then_inc(T.sem.lw, 16)
     PK, LX, LW = ("lpk", 16), [("lxa", 16), ("lxb", 16)], ("lw", 16)
 
     t_ones = tick("V", v.memset(T.ones[:], 1.0))
-    t_part = tick("G", g.iota(T.part[:], [[0, 1]], 0, 1))
+    for l in "oa":
+        t_zero = tick("V", v.memset(T[l + "u"][:], 0.0))
     wait("G", t_ones)
-    t_id = tick("G", g.affine_select(T.ident[:], T.ones[:], [[-1, 128]], AluOpType.is_equal, 0.0, 0, 1))
-    wait("V", t_part)
-    a = tick("V", v.tensor_scalar(T.hbit[:], T.part[:], 0, 1, AluOpType.arith_shift_right, AluOpType.bitwise_and))
-    wait("V", a)
-    tick("V", v.tensor_scalar(T.m1[:], T.hbit[:], 1.0, None, AluOpType.mult))
-    tick("V", v.tensor_scalar(T.m0[:], T.hbit[:], -1.0, 1.0, AluOpType.mult, AluOpType.add))
+    t_id = tick("G", g.affine_select(T.ident[:], T.ones[:], [[-1, 128]], A.is_equal, 0.0, 0, 1))
+
+    def shares(l, hi, lo, sh):
+        tick("V", v.tensor_scalar(T[l + "a"][:], T.pk[:], hi, None, A.bitwise_and))
+        tick("V", v.tensor_scalar(T[l + "b"][:], T.pk[:], lo, None, A.bitwise_and))
+        tick("V", v.tensor_scalar(T[l + "k"][:], T.pk[:], sh, 31, A.arith_shift_right, A.bitwise_and))
+
+    def scaled(l, s, mul):
+        tick("V", v.tensor_scalar(T[l + "1"][:], T[l + "a"][:], float(s), None, A.mult))
+        tick("V", v.tensor_scalar(T[l + "2"][:], T[l + "b"][:], float(mul), None, A.mult))
+
+    wait("V", PK)
+    shares("x", 0x700, 7, 3)
+    wait("V", now("V"))
+    scaled("x", 3, 96)
+    shares("w", 0x600, 15, 4)
+    wait("V", now("V"))
+    tick("V", v.tensor_tensor(T.x3[:], T.x1[:], T.x2[:], A.add))
+    scaled("w", 1, 32)
+    wait("V", now("V"))
+    t_fx = tick("V", v.tensor_tensor(T.fx[:], T.x3[:], T.xk[:], A.add))
+    tick("V", v.tensor_tensor(T.w3[:], T.w1[:], T.w2[:], A.add))
+    wait("V", now("V"))
+    t_fw = tick("V", v.tensor_tensor(T.fw[:], T.w3[:], T.wk[:], A.add))
 
     eng = [topo.engines(core, cores[s]) for s in D]
     picks = [eng[0][0:4], eng[1][4:8], eng[2][8:16]]
-    trs = []
-    for k, s in enumerate(D):
-        rid, pid, _ = topo.addr(cores[s])
-        dst = T.ld[:] if k == 0 else T.la[:, 4 * (k - 1):4 * k]
-        trs.append(RemoteDMATransfer(dst_ids=[DstId(rid=rid, pnc=pid)], dma_engine_mask=sum(1 << e for e in picks[k]),
-                                     remote_sem=T.sem["list%d" % k], src=T.pk[:, 4 * s:4 * s + 4], dst=dst))
+
+    def transfer(k, src, dst):
+        rid, pid, _ = topo.addr(cores[D[k]])
+        return RemoteDMATransfer(dst_ids=[DstId(rid=rid, pnc=pid)], dma_engine_mask=sum(1 << e for e in picks[k]),
+                                 remote_sem=T.sem["list%d" % k], src=src, dst=dst)
     wait("G", PK)
-    g.remote_dma_fused(trs, local_sem=T.sem.sent)
-    sent = sum(len(e) for e in picks)
+    g.remote_dma_fused([transfer(0, T.pk[:, 4 * D[0]:4 * D[0] + 4], T.ld[:])], local_sem=T.sem.sent)
+    wait("G", t_fx)
+    g.remote_dma_fused([transfer(k, T.fx[:, 4 * D[k]:4 * D[k] + 4], T.la[:, k - 1, :]) for k in (1, 2)],
+                       local_sem=T.sem.sent)
     LIST = [("list%d" % k, len(picks[k])) for k in range(3)]
 
     def gather(k, idx, t):
         g.indirect_dma_start(T["xg%d" % k][:, XC * t:XC * t + XC], None, T.x[:],
                              IndirectOffsetOnAxis(ap=idx, axis=0), bounds_check=R - 1).then_inc(T.sem["ig%d%d" % (k, t)], 16)
 
-    def own(t):
-        gather(1, T.pk[:, 4 * me + t:4 * me + t + 1], t)
+    def copy(q, out, in_):
+        if q == "V":
+            return tick("V", v.tensor_copy(out, in_))
+        return tick("S", sc.activation(out, in_, COPY))
 
-    own(0)
-    own(1)
-    wait("G", LIST[0])
-    for t in range(4):
-        gather(0, T.ld[:, t:t + 1], t)
-    own(2)
-
-    def list_front(p, src, n, hi, lo, sh, mul, s3):
-        b = lambda x: T[p + x]
-        tick("V", v.tensor_scalar(b("a1")[:], src, hi, None, AluOpType.bitwise_and))
-        tick("V", v.tensor_scalar(b("b1")[:], src, lo, None, AluOpType.bitwise_and))
-        tick("V", v.tensor_scalar(b("k1")[:], src, sh, 31, AluOpType.arith_shift_right, AluOpType.bitwise_and))
+    def spread(l, n, src, toks):
+        done = []
+        for m in range(4):
+            q = "VS"[m % 2]
+            wait(q, t_zero, *toks)
+            done.append(copy(q, T[l + "u"][:, m, 0:n, :], src))
+        wait("P", t_id, *done)
+        tok = tick("P", pe.transpose(T.pL[:, 0:128], T[l + "u"][:], T.ident[:]))
+        wait("S", tok)
+        a = copy("S", T[l + "d"][:, :, 0, :], T.pL[:, 0:128])
+        wait("V", a)
+        b = copy("V", T[l + "d"][:, :, 1, :], T.pL[:, 0:128])
+        wait("V", b)
+        for k in range(8):
+            tick("V", v.transpose(T[l + "z"][:, :, k], T[l + "d"][:, k, :, :]))
         wait("V", now("V"))
-        tick("V", v.tensor_scalar(b("f1")[:], b("a1")[:], float(s3), None, AluOpType.mult))
-        tick("V", v.tensor_scalar(b("f2")[:], b("b1")[:], float(mul), None, AluOpType.mult))
-        wait("V", now("V"))
-        tick("V", v.tensor_tensor(b("f3")[:], b("f1")[:], b("f2")[:], AluOpType.add))
-        wait("V", now("V"))
-        for h in range(2):
-            tick("V", v.tensor_tensor(b("u")[:, 0, :, :, h], b("f3")[:], b("k1")[:], AluOpType.add))
-        w = 1
-        while w < 16 // n:
-            wait("V", now("V"))
-            tick("V", v.tensor_copy(b("u")[:, w:2 * w], b("u")[:, 0:w]))
-            w *= 2
-        wait("P", now("V"), t_id)
-        return tick("P", pe.transpose(T.pL[:, 0:128], b("u")[:], T.ident[:]))
-
-    def list_back(p, n, tok):
-        b = lambda x: T[p + x]
-        wait("V", tok)
-        tick("V", v.tensor_scalar(b("e0")[:], T.pL[:, 0:128], T.m0[:], None, AluOpType.mult))
-        tick("V", v.tensor_scalar(b("e1")[:], T.pL[:, 0:128], T.m1[:], None, AluOpType.mult))
-        wait("V", now("V"))
-        for h in range(2):
-            tick("V", v.tensor_tensor(b("t2")[:, :, h, :], b("e0")[:, :, 0, :], b("e1")[:, :, 1, :], AluOpType.add))
-        wait("V", now("V"))
-        tick("V", v.transpose(b("z")[:], b("t2")[:]))
-        wait("V", now("V"))
-        for q in range(4):
-            tick("V", v.tensor_copy(b("om")[:, :, :, q, :], b("z")[:, q, 0:8 * n]))
-        wait("V", now("V"))
-        tick("V", v.tensor_copy(b("off")[:], b("om")[:]))
-        return now("V")
+        return tick("V", v.tensor_copy(T[l + "off"][:], T[l + "z"][:, 0:4 * n, :]))
 
     def turn_x(c):
         wait("V", LX[c])
@@ -192,26 +191,10 @@ def rank_program(g, core, T, topo):
                                 T.stg[32 * a:32 * a + 32, (4 * c + q) * XSLOT:(4 * c + q + 1) * XSLOT]
                                 ).then_inc(T.sem["xsh%d%d" % (c, d)], 16)
 
-    def turn_w():
-        wait("V", LW)
-        for q in range(4):
-            tick("V", v.transpose(T.wst[:, q * WSLOT:q * WSLOT + WSLOT], T.wn[:, :, 32 * q:32 * q + 32]))
-        wait("Y", now("V"))
-        for q in range(4):
-            for a in range(4):
-                sy.dma_start(T.ww[32 * q:32 * q + 32, a * WSLOT:(a + 1) * WSLOT],
-                             T.wst[32 * a:32 * a + 32, q * WSLOT:(q + 1) * WSLOT]).then_inc(T.sem.wsh, 16)
-
-    wait("V", PK)
-    tw = list_front("ow", T.pk[:], 4, 0x600, 15, 4, 32, 1)
+    t_offo = spread("o", 4, T.fw[:], [t_fw])
     turn_x(0)
-    t_offw = list_back("ow", 4, tw)
     turn_x(1)
-    turn_w()
-    wait("V", LIST[1], LIST[2])
-    wait("P", t_offw)
-    tx = list_front("ax", T.la[:], 2, 0x700, 7, 3, 96, 3)
-    t_offx = list_back("ax", 2, tx)
+    t_offa = spread("a", 2, T.la[:], LIST[1:3])
     XSH = [("xsh%d%d" % (c, d), 128) for c in range(2) for d in range(2)]
     WSH = ("wsh", 256)
 
@@ -220,88 +203,120 @@ def rank_program(g, core, T, topo):
             return tick("V", v.tensor_copy(out, win.indirect(off)))
         return tick("S", sc.activation(out, win.indirect(off), COPY))
 
-    def copy(q, out, in_):
-        if q == "V":
-            return tick("V", v.tensor_copy(out, in_))
-        return tick("S", sc.activation(out, in_, COPY))
+    tok = {}
+    held = {}
+    place = {}
+    turn = {"pX": 0, "pW": 0, "pY": 0}
+    sums = {"sent": sum(len(e) for e in picks), "y": 0}
 
-    free = {}
+    def bank(ps, n):
+        b = turn[ps] % n
+        turn[ps] += 1
+        return b
 
-    def through(q, ps, bank, buf, tok, out):
-        key = (ps, bank)
-        wait("P", t_id, tok, *([free[key]] if key in free else []))
+    def turned(task, ps, n, buf):
+        b = bank(ps, n)
+        wait("P", t_id, tok["g" + task[1:]], *([tok[held[(ps, b)]]] if (ps, b) in held else []))
         for t in range(4):
-            tick("P", pe.transpose(T[ps][:, 512 * bank + t:512 * bank + 512:4], buf[:, 128 * t:128 * t + 128], T.ident[:]))
-        wait(q, now("P"))
-        free[key] = copy(q, out, T[ps][:, 512 * bank:512 * bank + 512])
-        return free[key]
+            tick("P", pe.transpose(T[ps][:, 512 * b + t:512 * b + 512:4], buf[:, 128 * t:128 * t + 128], T.ident[:]))
+        held[(ps, b)] = "e" + task[1:]
+        tok[task] = now("P")
+        place[task] = b
 
-    def xtake(q, k, b):
-        wait(q, t_offx, *XSH)
-        return take(q, T["gx%d%d" % (k, b)][:], T.xw[:, 32 * b:32 * b + XW - 64], T.axoff[:, 32 * k:32 * k + 32])
+    def emptied(q, task, ps, out):
+        b = place["p" + task[1:]]
+        wait(q, tok["p" + task[1:]])
+        tok[task] = copy(q, out, T[ps][:, 512 * b:512 * b + 512])
 
-    def wtake(q, k):
-        wait(q, t_offw, WSH)
-        return take(q, T["gw%d" % k][:], T.ww[:], T.owoff[:, 32 * k:32 * k + 32])
+    def run(q, task):
+        kind, k, i = task[0], task[1], int(task[2:] or 0)
+        if task == "lw":
+            Q[q].dma_start(T.wn[:], T.w[:]).then_inc(T.sem.lw, 16)
+        elif task == "tw":
+            wait("V", LW)
+            for b in range(4):
+                tok[task] = tick("V", v.transpose(T.wst[:, b * WSLOT:b * WSLOT + WSLOT], T.wn[:, :, 32 * b:32 * b + 32]))
+        elif task == "cw":
+            wait(q, tok["tw"])
+            for b in range(4):
+                for a in range(4):
+                    Q[q].dma_start(T.ww[32 * b:32 * b + 32, a * WSLOT:(a + 1) * WSLOT],
+                                   T.wst[32 * a:32 * a + 32, b * WSLOT:(b + 1) * WSLOT]).then_inc(T.sem.wsh, 16)
+        elif kind == "g" and k == "w":
+            wait(q, t_offo, WSH)
+            tok[task] = take(q, T["gw%d" % i][:], T.ww[:], T.ooff[:, 32 * i:32 * i + 32])
+        elif kind == "g":
+            wait(q, t_offa, *XSH)
+            out = T["gx%d" % i][:] if k == "1" else T.gb[:, i, :]
+            tok[task] = take(q, out, T.xw[:, 32 * i:32 * i + XW - 64], T.aoff[:, 32 * int(k) - 32:32 * int(k)])
+        elif kind == "p" and k == "w":
+            turned(task, "pW", 2, T["gw%d" % i])
+        elif kind == "p":
+            turned(task, "pX", 3, T["gx%d" % i])
+        elif kind == "e" and k == "w":
+            emptied(q, task, "pW", T.wt[:, 512 * i:512 * i + 512])
+        elif kind == "e":
+            emptied(q, task, "pX", T.xt1[:, 512 * i:512 * i + 512])
+        elif task == "m2":
+            wait("V", *[tok["g2%d" % b] for b in range(3)])
+            for t in range(4):
+                tok[task] = tick("V", v.transpose(T.mv[:, :, :, :, t], T.gb[:, :, 128 * t:128 * t + 128]))
+        elif task == "d2":
+            wait(q, tok["m2"])
+            for a in range(4):
+                for b in range(4):
+                    Q[q].dma_start(T.xt2[32 * b:32 * b + 32, :, 128 * a:128 * a + 128],
+                                   T.mv[32 * a:32 * a + 32, :, b, :, :]).then_inc(T.sem.xm, 16)
+        elif kind == "l":
+            buf = "01"[k == "3"]
+            wait(q, ("ig%s%d" % (buf, i), 16))
+            tok[task] = copy(q, T["xt" + k][:, i:4 * XC:4], T["xg" + buf][:, XC * i:XC * i + XC])
+        elif task == "q2":
+            wait("V", ("xm", 256))
+            for b in range(3):
+                tok[task] = tick("V", v.quantize_mx(T.xq2[:, 128 * b:128 * b + 128], T.xs2[:, 128 * b:128 * b + 128],
+                                                    T.xt2[:, b, :]))
+        elif task == "qw":
+            wait("V", *[tok["ew%d" % b] for b in range(4)])
+            tok[task] = tick("V", v.quantize_mx(T.wq[:], T.ws[:], T.wt[:]))
+        elif kind == "q":
+            wait("V", *([tok["e1%d" % b] for b in range(3)] if k == "1" else [tok["l%s%d" % (k, t)] for t in range(4)]))
+            tok[task] = tick("V", v.quantize_mx(T["xq" + k][:], T["xs" + k][:], T["xt" + k][:]))
+        elif kind == "o":
+            t = int(k)
+            gather(1, T.pk[:, 4 * me + t:4 * me + t + 1], t)
+        elif kind == "i":
+            wait("G", LIST[0])
+            for t in range(4):
+                gather(0, T.ld[:, t:t + 1], t)
+        elif kind == "s":
+            c = cores[D[int(k)]]
+            rid, pid, _ = topo.addr(c)
+            wait("G", tok["q" + k])
+            g.remote_dma(T["rq" + k][:].bitcast(dt.uint8), T["xq" + k][:].bitcast(dt.uint8), T.sem["arr" + k], T.sem.sent,
+                         pid, rid, topo.mask(core, c))
+            g.remote_dma(T["rs" + k][:], T["xs" + k][:], T.sem["arr" + k], T.sem.sent, pid, rid, topo.mask(core, c))
+            sums["sent"] += 2 * len(eng[int(k)])
+        elif kind == "y":
+            s = (D + [me])[int(k)]
+            if k == "3":
+                xq, xs, arrived = T.xq3, T.xs3, tok["q3"]
+            else:
+                xq, xs, arrived = T["rq" + k], T["rs" + k], ("arr" + k, 2 * len(eng[int(k)]))
+            b = bank("pY", 2)
+            wait("P", tok["qw"], arrived, *([held[("pY", b)]] if ("pY", b) in held else []))
+            m = tick("P", pe.matmul_mx(T.pY[:, 512 * b:512 * b + XC], T.wq[:, 128 * s:128 * s + 128],
+                                       T.ws[:, 128 * s:128 * s + 128], xq[:], xs[:], True, True))
+            wait(q, m)
+            held[("pY", b)] = e = copy(q, T.ysb[:, XC * s:XC * s + XC], T.pY[:, 512 * b:512 * b + XC])
+            wait("Y", e)
+            sy.dma_start(T.y[:, XC * s:XC * s + XC], T.ysb[:, XC * s:XC * s + XC]).then_inc(T.sem["ys%d" % sums["y"]], 16)
+            sums["y"] += 1
 
-    def xthrough(q, k, b, bank, tok):
-        return through(q, "pX", bank, T["gx%d%d" % (k, b)], tok, T["xt%d" % (k + 1)][:, 512 * b:512 * b + 512])
-
-    def lace(k, buf, t):
-        wait("V", ("ig%d%d" % (buf, t), 16))
-        return tick("V", v.tensor_copy(T["xt%d" % k][:, t:4 * XC:4], T["xg%d" % buf][:, XC * t:XC * t + XC]))
-
-    def quant(k, *toks):
-        wait("V", *toks)
-        return tick("V", v.quantize_mx(T["xq%d" % k][:], T["xs%d" % k][:], T["xt%d" % k][:]))
-
-    gs = [xtake("S", 0, 0), xtake("S", 0, 1)]
-    gv = [xtake("V", 1, b) for b in range(3)]
-    for t in range(3):
-        lace(0, 0, t)
-    xthrough("S", 0, 0, 0, gs[0])
-    gs.append(xtake("S", 0, 2))
-    xthrough("V", 1, 0, 1, gv[0])
-    xthrough("S", 0, 1, 2, gs[1])
-    xthrough("V", 1, 1, 0, gv[1])
-    q0 = quant(0, lace(0, 0, 3))
-    q1 = quant(1, xthrough("S", 0, 2, 1, gs[2]))
-    q2 = quant(2, xthrough("V", 1, 2, 2, gv[2]))
-
-    for k, tok in enumerate((q0, q1, q2)):
-        c = cores[D[k]]
-        rid, pid, _ = topo.addr(c)
-        wait("G", tok)
-        g.remote_dma(T["rq%d" % k][:].bitcast(dt.uint8), T["xq%d" % k][:].bitcast(dt.uint8), T.sem["arr%d" % k], T.sem.sent,
-                     pid, rid, topo.mask(core, c))
-        g.remote_dma(T["rs%d" % k][:], T["xs%d" % k][:], T.sem["arr%d" % k], T.sem.sent, pid, rid, topo.mask(core, c))
-        sent += 2 * len(eng[k])
-    own(3)
-
-    tw = [wtake("S", k) for k in range(4)]
-    for t in range(3):
-        lace(3, 1, t)
-    tiles = [through("V", "pW", k % 2, T["gw%d" % k], tw[k], T.wt[:, 512 * k:512 * k + 512]) for k in range(4)]
-    wait("V", *tiles)
-    qw = tick("V", v.quantize_mx(T.wq[:], T.ws[:], T.wt[:]))
-    q3 = quant(3, lace(3, 1, 3))
-
-    for i, k in enumerate((2, 0, 3, 1)):
-        s = (D + [me])[k]
-        if k == 3:
-            xq, xs, tok = T.xq3, T.xs3, q3
-        else:
-            xq, xs, tok = T["rq%d" % k], T["rs%d" % k], ("arr%d" % k, 2 * len(eng[k]))
-        bank = 512 * (i % 2)
-        wait("P", qw, tok, *([free[("pY", bank)]] if i > 1 else []))
-        m = tick("P", pe.matmul_mx(T.pY[:, bank:bank + XC], T.wq[:, 128 * s:128 * s + 128], T.ws[:, 128 * s:128 * s + 128],
-                                   xq[:], xs[:], True, True))
-        q = "SV"[i % 2]
-        wait(q, m)
-        free[("pY", bank)] = e = copy(q, T.ysb[:, XC * s:XC * s + XC], T.pY[:, bank:bank + XC])
-        wait("Y", e)
-        sy.dma_start(T.y[:, XC * s:XC * s + XC], T.ysb[:, XC * s:XC * s + XC]).then_inc(T.sem["ys%d" % i], 16)
+    for step in PLAN.split():
+        q, task = step.split(":")
+        run(q, task)
     for i in range(4):
         wait("Y", ("ys%d" % i, 16))
     wait("Y", now("V"), now("S"), now("P"), now("G"))
-    wait("G", ("sent", sent))
+    wait("G", ("sent", sums["sent"]))

from concourse.bass import DstId, IndirectOffsetOnAxis, RemoteDMATransfer
from concourse.mybir import dt, AluOpType, ActivationFunctionType

N, R, XC = 4, 2048, 384
COPY = ActivationFunctionType.Copy
XW = 6144
XSLOT = 768
WSLOT = 512

PLAN = """
G:o1 G:i0 G:o0 G:o2
Y:lw S:g12 P:p12 S:g20 V:g10 V:tw S:g22 V:g21 S:g11 P:p10 V:l00 P:p11 S:e10 V:m2 V:e11 S:l01 V:l02
S:gw0 P:pw0 V:l03 S:gw1 V:q0 G:s0 V:ew0 V:e12 S:gw3 P:pw1 V:q1 P:pw3 S:l31 S:gw2 Y:cw S:l30 V:ew1 P:pw2
Y:d2 V:ew3 V:q2 G:o3 S:l32 V:ew2 S:l33 V:qw S:y0 G:s1 V:q3 V:y3 V:y1 V:y2 G:s2
"""

SCRATCH = {
    "ones": ("sbuf", [128, 128], "float32"),
    "ident": ("sbuf", [128, 128], "float32"),
    "pk": ("sbuf", [128, 16], "int32"),
    "ld": ("sbuf", [128, 4], "int32"),
    "la": ("sbuf", [128, 2, 4], "float32"),
    "fx": ("sbuf", [128, 16], "float32"),
    "fw": ("sbuf", [128, 16], "float32"),
    "nat": ("sbuf", [128, 48, 128], "bfloat16"),
    "stg": ("sbuf", [128, XW], "bfloat16"),
    "xw": ("sbuf", [128, XW], "bfloat16"),
    "wn": ("sbuf", [128, 16, 128], "bfloat16"),
    "wst": ("sbuf", [128, 2048], "bfloat16"),
    "ww": ("sbuf", [128, 2048], "bfloat16"),
    "wt": ("sbuf", [128, 2048], "bfloat16"),
    "wq": ("sbuf", [128, 512], "float8_e4m3fn_x4"),
    "ws": ("sbuf", [128, 512], "uint8"),
    "gb": ("sbuf", [128, 3, 512], "bfloat16"),
    "mv": ("sbuf", [128, 3, 4, 32, 4], "bfloat16"),
    "ysb": ("sbuf", [128, 1536], "float32"),
    "pX": ("psum", [128, 1536], "float32"),
    "pW": ("psum", [128, 1024], "float32"),
    "pL": ("psum", [128, 512], "float32"),
    "pY": ("psum", [128, 1024], "float32"),
}
for _b in ("xa", "xb", "xk", "wa", "wb", "wk"):
    SCRATCH[_b] = ("sbuf", [128, 16], "int32")
for _b in ("x1", "x2", "x3", "w1", "w2", "w3"):
    SCRATCH[_b] = ("sbuf", [128, 16], "float32")
for _l, _n in (("o", 4), ("a", 2)):
    SCRATCH[_l + "u"] = ("sbuf", [128, 4, 8, 4], "float32")
    SCRATCH[_l + "d"] = ("sbuf", [128, 8, 2, 16], "float32")
    SCRATCH[_l + "z"] = ("sbuf", [128, 32, 8], "float32")
    SCRATCH[_l + "off"] = ("sbuf", [128, 32 * _n], "uint16")
for _k in range(2):
    SCRATCH["xg%d" % _k] = ("sbuf", [128, 4 * XC], "bfloat16")
for _b in range(3):
    SCRATCH["gx%d" % _b] = ("sbuf", [128, 512], "float32")
    SCRATCH["rq%d" % _b] = ("sbuf", [128, XC], "float8_e4m3fn_x4")
    SCRATCH["rs%d" % _b] = ("sbuf", [128, XC], "uint8")
for _k in range(4):
    SCRATCH["gw%d" % _k] = ("sbuf", [128, 512], "float32")
    SCRATCH["xt%d" % _k] = ("sbuf", [128, 3, 512] if _k == 2 else [128, 4 * XC], "bfloat16")
    SCRATCH["xq%d" % _k] = ("sbuf", [128, XC], "float8_e4m3fn_x4")
    SCRATCH["xs%d" % _k] = ("sbuf", [128, XC], "uint8")

SEMAPHORES = (["V", "S", "P", "G", "sent", "lpk", "lxa", "lxb", "lw", "wsh", "xm"]
              + ["xsh%d%d" % (c, q) for c in range(2) for q in range(2)]
              + ["list%d" % k for k in range(3)] + ["arr%d" % k for k in range(3)]
              + ["ig%d%d" % (k, t) for k in range(2) for t in range(4)]
              + ["ys%d" % k for k in range(4)])


def roles(core, T, topo):
    me = T.rank_of(core)
    far = [s for s in range(N) if topo.chip(T.cores[s]) != topo.chip(core)]
    far.sort(key=lambda s: topo.die(T.cores[s]) != topo.die(core))
    return far + [s for s in range(N) if s != me and s not in far]


def rank_program(g, core, T, topo):
    me = T.rank_of(core)
    if me is None:
        return
    Q = {"V": g.vector, "S": g.scalar, "P": g.tensor, "G": g, "Y": g.sync}
    count = {"V": 0, "S": 0, "P": 0, "G": 0}
    seen = {}

    def wait(q, *toks):
        for name, val in toks:
            if seen.get((q, name), 0) < val:
                seen[(q, name)] = val
                Q[q].wait_ge(T.sem[name], val)

    def tick(q, ins):
        count[q] += 1
        ins.then_inc(T.sem[q], 1)
        return (q, count[q])

    def now(q):
        return (q, count[q])

    v, sc, pe, sy = g.vector, g.scalar, g.tensor, g.sync
    D = roles(core, T, topo)
    cores = T.cores
    A = AluOpType

    sc.dma_start(T.pk[:], T.pick[:]).then_inc(T.sem.lpk, 16)
    sy.dma_start(T.nat[:, 0:24, :], T.x[0:1024, :]).then_inc(T.sem.lxa, 16)
    sy.dma_start(T.nat[:, 24:48, :], T.x[1024:2048, :]).then_inc(T.sem.lxb, 16)
    PK, LX, LW = ("lpk", 16), [("lxa", 16), ("lxb", 16)], ("lw", 16)

    t_ones = tick("V", v.memset(T.ones[:], 1.0))
    for l in "oa":
        t_zero = tick("V", v.memset(T[l + "u"][:], 0.0))
    wait("G", t_ones)
    t_id = tick("G", g.affine_select(T.ident[:], T.ones[:], [[-1, 128]], A.is_equal, 0.0, 0, 1))

    def shares(l, hi, lo, sh):
        tick("V", v.tensor_scalar(T[l + "a"][:], T.pk[:], hi, None, A.bitwise_and))
        tick("V", v.tensor_scalar(T[l + "b"][:], T.pk[:], lo, None, A.bitwise_and))
        tick("V", v.tensor_scalar(T[l + "k"][:], T.pk[:], sh, 31, A.arith_shift_right, A.bitwise_and))

    def scaled(l, s, mul):
        tick("V", v.tensor_scalar(T[l + "1"][:], T[l + "a"][:], float(s), None, A.mult))
        tick("V", v.tensor_scalar(T[l + "2"][:], T[l + "b"][:], float(mul), None, A.mult))

    wait("V", PK)
    shares("x", 0x700, 7, 3)
    wait("V", now("V"))
    scaled("x", 3, 96)
    shares("w", 0x600, 15, 4)
    wait("V", now("V"))
    tick("V", v.tensor_tensor(T.x3[:], T.x1[:], T.x2[:], A.add))
    scaled("w", 1, 32)
    wait("V", now("V"))
    t_fx = tick("V", v.tensor_tensor(T.fx[:], T.x3[:], T.xk[:], A.add))
    tick("V", v.tensor_tensor(T.w3[:], T.w1[:], T.w2[:], A.add))
    wait("V", now("V"))
    t_fw = tick("V", v.tensor_tensor(T.fw[:], T.w3[:], T.wk[:], A.add))

    eng = [topo.engines(core, cores[s]) for s in D]
    picks = [eng[0][0:4], eng[1][4:8], eng[2][8:16]]

    def transfer(k, src, dst):
        rid, pid, _ = topo.addr(cores[D[k]])
        return RemoteDMATransfer(dst_ids=[DstId(rid=rid, pnc=pid)], dma_engine_mask=sum(1 << e for e in picks[k]),
                                 remote_sem=T.sem["list%d" % k], src=src, dst=dst)
    wait("G", PK)
    g.remote_dma_fused([transfer(0, T.pk[:, 4 * D[0]:4 * D[0] + 4], T.ld[:])], local_sem=T.sem.sent)
    wait("G", t_fx)
    g.remote_dma_fused([transfer(k, T.fx[:, 4 * D[k]:4 * D[k] + 4], T.la[:, k - 1, :]) for k in (1, 2)],
                       local_sem=T.sem.sent)
    LIST = [("list%d" % k, len(picks[k])) for k in range(3)]

    def gather(k, idx, t):
        g.indirect_dma_start(T["xg%d" % k][:, XC * t:XC * t + XC], None, T.x[:],
                             IndirectOffsetOnAxis(ap=idx, axis=0), bounds_check=R - 1).then_inc(T.sem["ig%d%d" % (k, t)], 16)

    def copy(q, out, in_):
        if q == "V":
            return tick("V", v.tensor_copy(out, in_))
        return tick("S", sc.activation(out, in_, COPY))

    def spread(l, n, src, toks):
        done = []
        for m in range(4):
            q = "VS"[m % 2]
            wait(q, t_zero, *toks)
            done.append(copy(q, T[l + "u"][:, m, 0:n, :], src))
        wait("P", t_id, *done)
        tok = tick("P", pe.transpose(T.pL[:, 0:128], T[l + "u"][:], T.ident[:]))
        wait("S", tok)
        a = copy("S", T[l + "d"][:, :, 0, :], T.pL[:, 0:128])
        wait("V", a)
        b = copy("V", T[l + "d"][:, :, 1, :], T.pL[:, 0:128])
        wait("V", b)
        for k in range(8):
            tick("V", v.transpose(T[l + "z"][:, :, k], T[l + "d"][:, k, :, :]))
        wait("V", now("V"))
        return tick("V", v.tensor_copy(T[l + "off"][:], T[l + "z"][:, 0:4 * n, :]))

    def turn_x(c):
        wait("V", LX[c])
        toks = []
        for q in range(4):
            o = (4 * c + q) * XSLOT
            toks.append(tick("V", v.transpose(T.stg[:, o:o + XSLOT], T.nat[:, 24 * c:24 * c + 24, 32 * q:32 * q + 32])))
        for q in range(4):
            for a in range(4):
                d = a % 2
                qq = ("Y", "S")[d]
                wait(qq, toks[q])
                Q[qq].dma_start(T.xw[32 * q:32 * q + 32, (4 * c + a) * XSLOT:(4 * c + a + 1) * XSLOT],
                                T.stg[32 * a:32 * a + 32, (4 * c + q) * XSLOT:(4 * c + q + 1) * XSLOT]
                                ).then_inc(T.sem["xsh%d%d" % (c, d)], 16)

    t_offo = spread("o", 4, T.fw[:], [t_fw])
    turn_x(0)
    turn_x(1)
    t_offa = spread("a", 2, T.la[:], LIST[1:3])
    XSH = [("xsh%d%d" % (c, d), 128) for c in range(2) for d in range(2)]
    WSH = ("wsh", 256)

    def take(q, out, win, off):
        if q == "V":
            return tick("V", v.tensor_copy(out, win.indirect(off)))
        return tick("S", sc.activation(out, win.indirect(off), COPY))

    tok = {}
    held = {}
    place = {}
    turn = {"pX": 0, "pW": 0, "pY": 0}
    sums = {"sent": sum(len(e) for e in picks), "y": 0}

    def bank(ps, n):
        b = turn[ps] % n
        turn[ps] += 1
        return b

    def turned(task, ps, n, buf):
        b = bank(ps, n)
        wait("P", t_id, tok["g" + task[1:]], *([tok[held[(ps, b)]]] if (ps, b) in held else []))
        for t in range(4):
            tick("P", pe.transpose(T[ps][:, 512 * b + t:512 * b + 512:4], buf[:, 128 * t:128 * t + 128], T.ident[:]))
        held[(ps, b)] = "e" + task[1:]
        tok[task] = now("P")
        place[task] = b

    def emptied(q, task, ps, out):
        b = place["p" + task[1:]]
        wait(q, tok["p" + task[1:]])
        tok[task] = copy(q, out, T[ps][:, 512 * b:512 * b + 512])

    def run(q, task):
        kind, k, i = task[0], task[1], int(task[2:] or 0)
        if task == "lw":
            Q[q].dma_start(T.wn[:], T.w[:]).then_inc(T.sem.lw, 16)
        elif task == "tw":
            wait("V", LW)
            for b in range(4):
                tok[task] = tick("V", v.transpose(T.wst[:, b * WSLOT:b * WSLOT + WSLOT], T.wn[:, :, 32 * b:32 * b + 32]))
        elif task == "cw":
            wait(q, tok["tw"])
            for b in range(4):
                for a in range(4):
                    Q[q].dma_start(T.ww[32 * b:32 * b + 32, a * WSLOT:(a + 1) * WSLOT],
                                   T.wst[32 * a:32 * a + 32, b * WSLOT:(b + 1) * WSLOT]).then_inc(T.sem.wsh, 16)
        elif kind == "g" and k == "w":
            wait(q, t_offo, WSH)
            tok[task] = take(q, T["gw%d" % i][:], T.ww[:], T.ooff[:, 32 * i:32 * i + 32])
        elif kind == "g":
            wait(q, t_offa, *XSH)
            out = T["gx%d" % i][:] if k == "1" else T.gb[:, i, :]
            tok[task] = take(q, out, T.xw[:, 32 * i:32 * i + XW - 64], T.aoff[:, 32 * int(k) - 32:32 * int(k)])
        elif kind == "p" and k == "w":
            turned(task, "pW", 2, T["gw%d" % i])
        elif kind == "p":
            turned(task, "pX", 3, T["gx%d" % i])
        elif kind == "e" and k == "w":
            emptied(q, task, "pW", T.wt[:, 512 * i:512 * i + 512])
        elif kind == "e":
            emptied(q, task, "pX", T.xt1[:, 512 * i:512 * i + 512])
        elif task == "m2":
            wait("V", *[tok["g2%d" % b] for b in range(3)])
            for t in range(4):
                tok[task] = tick("V", v.transpose(T.mv[:, :, :, :, t], T.gb[:, :, 128 * t:128 * t + 128]))
        elif task == "d2":
            wait(q, tok["m2"])
            for a in range(4):
                for b in range(4):
                    Q[q].dma_start(T.xt2[32 * b:32 * b + 32, :, 128 * a:128 * a + 128],
                                   T.mv[32 * a:32 * a + 32, :, b, :, :]).then_inc(T.sem.xm, 16)
        elif kind == "l":
            buf = "01"[k == "3"]
            wait(q, ("ig%s%d" % (buf, i), 16))
            tok[task] = copy(q, T["xt" + k][:, i:4 * XC:4], T["xg" + buf][:, XC * i:XC * i + XC])
        elif task == "q2":
            wait("V", ("xm", 256))
            for b in range(3):
                tok[task] = tick("V", v.quantize_mx(T.xq2[:, 128 * b:128 * b + 128], T.xs2[:, 128 * b:128 * b + 128],
                                                    T.xt2[:, b, :]))
        elif task == "qw":
            wait("V", *[tok["ew%d" % b] for b in range(4)])
            tok[task] = tick("V", v.quantize_mx(T.wq[:], T.ws[:], T.wt[:]))
        elif kind == "q":
            wait("V", *([tok["e1%d" % b] for b in range(3)] if k == "1" else [tok["l%s%d" % (k, t)] for t in range(4)]))
            tok[task] = tick("V", v.quantize_mx(T["xq" + k][:], T["xs" + k][:], T["xt" + k][:]))
        elif kind == "o":
            t = int(k)
            gather(1, T.pk[:, 4 * me + t:4 * me + t + 1], t)
        elif kind == "i":
            wait("G", LIST[0])
            for t in range(4):
                gather(0, T.ld[:, t:t + 1], t)
        elif kind == "s":
            c = cores[D[int(k)]]
            rid, pid, _ = topo.addr(c)
            wait("G", tok["q" + k])
            g.remote_dma(T["rq" + k][:].bitcast(dt.uint8), T["xq" + k][:].bitcast(dt.uint8), T.sem["arr" + k], T.sem.sent,
                         pid, rid, topo.mask(core, c))
            g.remote_dma(T["rs" + k][:], T["xs" + k][:], T.sem["arr" + k], T.sem.sent, pid, rid, topo.mask(core, c))
            sums["sent"] += 2 * len(eng[int(k)])
        elif kind == "y":
            s = (D + [me])[int(k)]
            if k == "3":
                xq, xs, arrived = T.xq3, T.xs3, tok["q3"]
            else:
                xq, xs, arrived = T["rq" + k], T["rs" + k], ("arr" + k, 2 * len(eng[int(k)]))
            b = bank("pY", 2)
            wait("P", tok["qw"], arrived, *([held[("pY", b)]] if ("pY", b) in held else []))
            m = tick("P", pe.matmul_mx(T.pY[:, 512 * b:512 * b + XC], T.wq[:, 128 * s:128 * s + 128],
                                       T.ws[:, 128 * s:128 * s + 128], xq[:], xs[:], True, True))
            wait(q, m)
            held[("pY", b)] = e = copy(q, T.ysb[:, XC * s:XC * s + XC], T.pY[:, 512 * b:512 * b + XC])
            wait("Y", e)
            sy.dma_start(T.y[:, XC * s:XC * s + XC], T.ysb[:, XC * s:XC * s + XC]).then_inc(T.sem["ys%d" % sums["y"]], 16)
            sums["y"] += 1

    for step in PLAN.split():
        q, task = step.split(":")
        run(q, task)
    for i in range(4):
        wait("Y", ("ys%d" % i, 16))
    wait("Y", now("V"), now("S"), now("P"), now("G"))
    wait("G", ("sent", sums["sent"]))
